import numpy as np
CORES = [32,40,160,168]
N = 4
def setup_inputs(rng):
    return {"x": rng.standard_normal((N, 128, 2048), dtype=np.float32)}
def reference(x):
    s = x.sum(axis=0, dtype=np.float64).astype(x.dtype)
    p = 128 // N
    return {"y": np.stack([s[r * p:(r + 1) * p, :] for r in range(N)])}

@@ -1,0 +1,109 @@
+from concourse.bass import DstId, RemoteDMATransfer
+from concourse.mybir import AluOpType
+
+W = 512
+NP = 1
+FOLD = (2,)
+RELAY = ()
+WP = W // NP
+RP = 32 // NP
+
+SCRATCH = {
+    "st": ("sbuf", [128, 3 * W], "float32"),
+    "in0": ("sbuf", [128, W], "float32"),
+    "in1": ("sbuf", [128, W], "float32"),
+}
+SEMAPHORES = (["y0", "sent"]
+              + [n + str(j) for j in range(4) for n in ("ldd", "lds", "ldm", "gota", "gotb", "acca", "accb")])
+
+
+def masks(lo, n, parts):
+    e = n // parts
+    return [((1 << e) - 1) << (lo + i * e) for i in range(parts)]
+
+
+def rank_program(g, core, T, topo):
+    k = core % 8
+    r = T.rank_of(core - k)
+    if r is None:
+        return
+    home, mate, peer = T.cores[r], T.cores[r ^ 1], T.cores[r ^ 2]
+    S = T.sem
+    ldd = [S.ldd0, S.ldd1, S.ldd2, S.ldd3]
+    lds = [S.lds0, S.lds1, S.lds2, S.lds3]
+    ldm = [S.ldm0, S.ldm1, S.ldm2, S.ldm3]
+    gota = [S.gota0, S.gota1, S.gota2, S.gota3]
+    gotb = [S.gotb0, S.gotb1, S.gotb2, S.gotb3]
+    acca = [S.acca0, S.acca1, S.acca2, S.acca3]
+    accb = [S.accb0, S.accb1, S.accb2, S.accb3]
+
+    def tr(dst, srcs, out, mask, rsem):
+        rid, pid = topo.addr(dst, core)
+        return RemoteDMATransfer(dst_ids=[DstId(rid=rid, pnc=pid)], dma_engine_mask=mask, remote_sem=rsem,
+                                 srcs=srcs, dsts=[out], alu_op=1 if len(srcs) > 1 else 0)
+
+    nf, nr = len(FOLD), len(RELAY)
+    wf = WP // nf
+
+    if k == 0:
+        sent = 0
+        for j in range(NP):
+            for b, (t, ld) in enumerate(((r ^ 3, ldd), (r ^ 2, lds), (r ^ 1, ldm))):
+                g.dma_start(out=T.st[:, b * W + j * WP:b * W + (j + 1) * WP],
+                            in_=T.x[32 * t + j * RP:32 * t + (j + 1) * RP, :]).then_inc(ld[j], 16)
+        g.dma_start(out=T.y[:, :], in_=T.x[32 * r:32 * r + 32, :]).then_inc(S.y0, 16)
+        for j in range(NP):
+            c0 = j * WP
+            g.wait_ge(ldd[j], 16)
+            ms = masks(0, 8, nf)
+            g.remote_dma_fused([tr(peer + f, [T.st[:, c0 + i * wf:c0 + (i + 1) * wf]],
+                                   T.in1[:, c0 + i * wf:c0 + (i + 1) * wf], ms[i], gotb[j])
+                                for i, f in enumerate(FOLD)], local_sem=S.sent)
+            sent += 8
+            g.wait_ge(lds[j], 16)
+            if nr:
+                wr = WP // nr
+                ms = masks(0, 16, nr)
+                g.remote_dma_fused([tr(home + f, [T.st[:, W + c0 + i * wr:W + c0 + (i + 1) * wr]],
+                                       T.in0[:, c0 + i * wr:c0 + (i + 1) * wr], ms[i], gota[j])
+                                    for i, f in enumerate(RELAY)], local_sem=S.sent)
+                sent += 16
+            else:
+                g.remote_dma_fused([tr(peer, [T.st[:, W + c0:W + c0 + WP]], T.in0[:, c0:c0 + WP], 0xFF, gota[j])],
+                                   local_sem=S.sent)
+                sent += 8
+            g.wait_ge(ldm[j], 16)
+            ms = masks(0, 16, nf)
+            g.remote_dma_fused([tr(home + f, [T.st[:, 2 * W + c0 + i * wf:2 * W + c0 + (i + 1) * wf]],
+                                   T.in0[:, c0 + i * wf:c0 + (i + 1) * wf], ms[i], gota[j])
+                                for i, f in enumerate(FOLD)], local_sem=S.sent)
+            sent += 16
+        g.wait_ge(S.y0, 16)
+        for j in range(NP):
+            g.wait_ge(gota[j], 8 * max(nr, 1))
+            g.dma_start(out=T.y[j * RP:(j + 1) * RP, :], in_=T.in0[:, j * WP:(j + 1) * WP],
+                        accum_op=AluOpType.add).then_inc(acca[j], 16)
+        for j in range(NP):
+            g.wait_ge(acca[j], 16)
+            g.wait_ge(gotb[j], 8 * nf)
+            g.dma_start(out=T.y[j * RP:(j + 1) * RP, :], in_=T.in1[:, j * WP:(j + 1) * WP],
+                        accum_op=AluOpType.add).then_inc(accb[j], 16)
+        for j in range(NP):
+            g.wait_ge(accb[j], 16)
+        g.wait_ge(S.sent, sent)
+    elif k in FOLD:
+        i = FOLD.index(k)
+        for j in range(NP):
+            c = slice(j * WP + i * wf, j * WP + (i + 1) * wf)
+            g.wait_ge(gota[j], 16 // nf)
+            g.wait_ge(gotb[j], 8 // nf)
+            g.remote_dma_fused([tr(mate, [T.in0[:, c], T.in1[:, c]], T.in1[:, c], 0xFF, gotb[j])], local_sem=S.sent)
+        g.wait_ge(S.sent, 8 * NP)
+    elif k in RELAY:
+        i = RELAY.index(k)
+        wr = WP // nr
+        for j in range(NP):
+            c = slice(j * WP + i * wr, j * WP + (i + 1) * wr)
+            g.wait_ge(gota[j], 16 // nr)
+            g.remote_dma_fused([tr(peer, [T.in0[:, c]], T.in0[:, c], 0xFF, gota[j])], local_sem=S.sent)
+        g.wait_ge(S.sent, 8 * NP)

@@ -3,7 +3,7 @@ from concourse.mybir import AluOpType
 
 W = 512
 NP = 1
-FOLD = (2,)
+FOLD = (2, 6)
 RELAY = ()
 WP = W // NP
 RP = 32 // NP

@@ -4,7 +4,7 @@ from concourse.mybir import AluOpType
 W = 512
 NP = 1
 FOLD = (2, 6)
-RELAY = ()
+RELAY = (4, 5)
 WP = W // NP
 RP = 32 // NP
 
@@ -51,7 +51,6 @@ def rank_program(g, core, T, topo):
             for b, (t, ld) in enumerate(((r ^ 3, ldd), (r ^ 2, lds), (r ^ 1, ldm))):
                 g.dma_start(out=T.st[:, b * W + j * WP:b * W + (j + 1) * WP],
                             in_=T.x[32 * t + j * RP:32 * t + (j + 1) * RP, :]).then_inc(ld[j], 16)
-        g.dma_start(out=T.y[:, :], in_=T.x[32 * r:32 * r + 32, :]).then_inc(S.y0, 16)
         for j in range(NP):
             c0 = j * WP
             g.wait_ge(ldd[j], 16)
@@ -63,21 +62,21 @@ def rank_program(g, core, T, topo):
             g.wait_ge(lds[j], 16)
             if nr:
                 wr = WP // nr
-                ms = masks(0, 16, nr)
+                ms = masks(8, 8, nr)
                 g.remote_dma_fused([tr(home + f, [T.st[:, W + c0 + i * wr:W + c0 + (i + 1) * wr]],
                                        T.in0[:, c0 + i * wr:c0 + (i + 1) * wr], ms[i], gota[j])
                                     for i, f in enumerate(RELAY)], local_sem=S.sent)
-                sent += 16
             else:
                 g.remote_dma_fused([tr(peer, [T.st[:, W + c0:W + c0 + WP]], T.in0[:, c0:c0 + WP], 0xFF, gota[j])],
                                    local_sem=S.sent)
-                sent += 8
+            sent += 8
             g.wait_ge(ldm[j], 16)
-            ms = masks(0, 16, nf)
+            ms = masks(8, 8, nf)
             g.remote_dma_fused([tr(home + f, [T.st[:, 2 * W + c0 + i * wf:2 * W + c0 + (i + 1) * wf]],
                                    T.in0[:, c0 + i * wf:c0 + (i + 1) * wf], ms[i], gota[j])
                                 for i, f in enumerate(FOLD)], local_sem=S.sent)
-            sent += 16
+            sent += 8
+        g.dma_start(out=T.y[:, :], in_=T.x[32 * r:32 * r + 32, :]).then_inc(S.y0, 16)
         g.wait_ge(S.y0, 16)
         for j in range(NP):
             g.wait_ge(gota[j], 8 * max(nr, 1))
@@ -95,7 +94,7 @@ def rank_program(g, core, T, topo):
         i = FOLD.index(k)
         for j in range(NP):
             c = slice(j * WP + i * wf, j * WP + (i + 1) * wf)
-            g.wait_ge(gota[j], 16 // nf)
+            g.wait_ge(gota[j], 8 // nf)
             g.wait_ge(gotb[j], 8 // nf)
             g.remote_dma_fused([tr(mate, [T.in0[:, c], T.in1[:, c]], T.in1[:, c], 0xFF, gotb[j])], local_sem=S.sent)
         g.wait_ge(S.sent, 8 * NP)
@@ -104,6 +103,6 @@ def rank_program(g, core, T, topo):
         wr = WP // nr
         for j in range(NP):
             c = slice(j * WP + i * wr, j * WP + (i + 1) * wr)
-            g.wait_ge(gota[j], 16 // nr)
+            g.wait_ge(gota[j], 8 // nr)
             g.remote_dma_fused([tr(peer, [T.in0[:, c]], T.in0[:, c], 0xFF, gota[j])], local_sem=S.sent)
         g.wait_ge(S.sent, 8 * NP)

@@ -2,24 +2,16 @@ from concourse.bass import DstId, RemoteDMATransfer
 from concourse.mybir import AluOpType
 
 W = 512
-NP = 1
+H = W // 2
 FOLD = (2, 6)
 RELAY = (4, 5)
-WP = W // NP
-RP = 32 // NP
 
 SCRATCH = {
     "st": ("sbuf", [128, 3 * W], "float32"),
     "in0": ("sbuf", [128, W], "float32"),
     "in1": ("sbuf", [128, W], "float32"),
 }
-SEMAPHORES = (["y0", "sent"]
-              + [n + str(j) for j in range(4) for n in ("ldd", "lds", "ldm", "gota", "gotb", "acca", "accb")])
-
-
-def masks(lo, n, parts):
-    e = n // parts
-    return [((1 << e) - 1) << (lo + i * e) for i in range(parts)]
+SEMAPHORES = ["ldd", "lds", "ldm", "y0", "acca", "accb", "gota", "gotb", "sent"]
 
 
 def rank_program(g, core, T, topo):
@@ -29,80 +21,44 @@ def rank_program(g, core, T, topo):
         return
     home, mate, peer = T.cores[r], T.cores[r ^ 1], T.cores[r ^ 2]
     S = T.sem
-    ldd = [S.ldd0, S.ldd1, S.ldd2, S.ldd3]
-    lds = [S.lds0, S.lds1, S.lds2, S.lds3]
-    ldm = [S.ldm0, S.ldm1, S.ldm2, S.ldm3]
-    gota = [S.gota0, S.gota1, S.gota2, S.gota3]
-    gotb = [S.gotb0, S.gotb1, S.gotb2, S.gotb3]
-    acca = [S.acca0, S.acca1, S.acca2, S.acca3]
-    accb = [S.accb0, S.accb1, S.accb2, S.accb3]
 
     def tr(dst, srcs, out, mask, rsem):
         rid, pid = topo.addr(dst, core)
         return RemoteDMATransfer(dst_ids=[DstId(rid=rid, pnc=pid)], dma_engine_mask=mask, remote_sem=rsem,
                                  srcs=srcs, dsts=[out], alu_op=1 if len(srcs) > 1 else 0)
 
-    nf, nr = len(FOLD), len(RELAY)
-    wf = WP // nf
+    def half(i, base=0):
+        return slice(base + i * H, base + (i + 1) * H)
 
     if k == 0:
-        sent = 0
-        for j in range(NP):
-            for b, (t, ld) in enumerate(((r ^ 3, ldd), (r ^ 2, lds), (r ^ 1, ldm))):
-                g.dma_start(out=T.st[:, b * W + j * WP:b * W + (j + 1) * WP],
-                            in_=T.x[32 * t + j * RP:32 * t + (j + 1) * RP, :]).then_inc(ld[j], 16)
-        for j in range(NP):
-            c0 = j * WP
-            g.wait_ge(ldd[j], 16)
-            ms = masks(0, 8, nf)
-            g.remote_dma_fused([tr(peer + f, [T.st[:, c0 + i * wf:c0 + (i + 1) * wf]],
-                                   T.in1[:, c0 + i * wf:c0 + (i + 1) * wf], ms[i], gotb[j])
-                                for i, f in enumerate(FOLD)], local_sem=S.sent)
-            sent += 8
-            g.wait_ge(lds[j], 16)
-            if nr:
-                wr = WP // nr
-                ms = masks(8, 8, nr)
-                g.remote_dma_fused([tr(home + f, [T.st[:, W + c0 + i * wr:W + c0 + (i + 1) * wr]],
-                                       T.in0[:, c0 + i * wr:c0 + (i + 1) * wr], ms[i], gota[j])
-                                    for i, f in enumerate(RELAY)], local_sem=S.sent)
-            else:
-                g.remote_dma_fused([tr(peer, [T.st[:, W + c0:W + c0 + WP]], T.in0[:, c0:c0 + WP], 0xFF, gota[j])],
-                                   local_sem=S.sent)
-            sent += 8
-            g.wait_ge(ldm[j], 16)
-            ms = masks(8, 8, nf)
-            g.remote_dma_fused([tr(home + f, [T.st[:, 2 * W + c0 + i * wf:2 * W + c0 + (i + 1) * wf]],
-                                   T.in0[:, c0 + i * wf:c0 + (i + 1) * wf], ms[i], gota[j])
-                                for i, f in enumerate(FOLD)], local_sem=S.sent)
-            sent += 8
+        for b, (t, ld) in enumerate(((r ^ 3, S.ldd), (r ^ 2, S.lds), (r ^ 1, S.ldm))):
+            g.dma_start(out=T.st[:, b * W:(b + 1) * W], in_=T.x[32 * t:32 * t + 32, :]).then_inc(ld, 16)
+        g.wait_ge(S.ldd, 16)
+        g.remote_dma_fused([tr(peer + f, [T.st[:, half(i)]], T.in1[:, half(i)], 0xF << (4 * i), S.gotb)
+                            for i, f in enumerate(FOLD)], local_sem=S.sent)
+        g.wait_ge(S.lds, 16)
+        g.remote_dma_fused([tr(home + f, [T.st[:, half(i, W)]], T.in0[:, half(i)], 0xF00 << (4 * i), S.gota)
+                            for i, f in enumerate(RELAY)], local_sem=S.sent)
+        g.wait_ge(S.ldm, 16)
+        g.remote_dma_fused([tr(home + f, [T.st[:, half(i, 2 * W)]], T.in0[:, half(i)], 0xF00 << (4 * i), S.gota)
+                            for i, f in enumerate(FOLD)], local_sem=S.sent)
         g.dma_start(out=T.y[:, :], in_=T.x[32 * r:32 * r + 32, :]).then_inc(S.y0, 16)
         g.wait_ge(S.y0, 16)
-        for j in range(NP):
-            g.wait_ge(gota[j], 8 * max(nr, 1))
-            g.dma_start(out=T.y[j * RP:(j + 1) * RP, :], in_=T.in0[:, j * WP:(j + 1) * WP],
-                        accum_op=AluOpType.add).then_inc(acca[j], 16)
-        for j in range(NP):
-            g.wait_ge(acca[j], 16)
-            g.wait_ge(gotb[j], 8 * nf)
-            g.dma_start(out=T.y[j * RP:(j + 1) * RP, :], in_=T.in1[:, j * WP:(j + 1) * WP],
-                        accum_op=AluOpType.add).then_inc(accb[j], 16)
-        for j in range(NP):
-            g.wait_ge(accb[j], 16)
-        g.wait_ge(S.sent, sent)
+        g.wait_ge(S.gota, 16)
+        g.dma_start(out=T.y[:, :], in_=T.in0[:, :], accum_op=AluOpType.add).then_inc(S.acca, 16)
+        g.wait_ge(S.acca, 16)
+        g.wait_ge(S.gotb, 16)
+        g.dma_start(out=T.y[:, :], in_=T.in1[:, :], accum_op=AluOpType.add).then_inc(S.accb, 16)
+        g.wait_ge(S.accb, 16)
+        g.wait_ge(S.sent, 24)
     elif k in FOLD:
-        i = FOLD.index(k)
-        for j in range(NP):
-            c = slice(j * WP + i * wf, j * WP + (i + 1) * wf)
-            g.wait_ge(gota[j], 8 // nf)
-            g.wait_ge(gotb[j], 8 // nf)
-            g.remote_dma_fused([tr(mate, [T.in0[:, c], T.in1[:, c]], T.in1[:, c], 0xFF, gotb[j])], local_sem=S.sent)
-        g.wait_ge(S.sent, 8 * NP)
+        c = half(FOLD.index(k))
+        g.wait_ge(S.gota, 4)
+        g.wait_ge(S.gotb, 4)
+        g.remote_dma_fused([tr(mate, [T.in0[:, c], T.in1[:, c]], T.in1[:, c], 0xFF, S.gotb)], local_sem=S.sent)
+        g.wait_ge(S.sent, 8)
     elif k in RELAY:
-        i = RELAY.index(k)
-        wr = WP // nr
-        for j in range(NP):
-            c = slice(j * WP + i * wr, j * WP + (i + 1) * wr)
-            g.wait_ge(gota[j], 8 // nr)
-            g.remote_dma_fused([tr(peer, [T.in0[:, c]], T.in0[:, c], 0xFF, gota[j])], local_sem=S.sent)
-        g.wait_ge(S.sent, 8 * NP)
+        c = half(RELAY.index(k))
+        g.wait_ge(S.gota, 4)
+        g.remote_dma_fused([tr(peer, [T.in0[:, c]], T.in0[:, c], 0xFF, S.gota)], local_sem=S.sent)
+        g.wait_ge(S.sent, 8)

from concourse.bass import DstId, RemoteDMATransfer
from concourse.mybir import AluOpType

W = 512
H = W // 2
FOLD = (2, 6)
RELAY = (4, 5)

SCRATCH = {
    "st": ("sbuf", [128, 3 * W], "float32"),
    "in0": ("sbuf", [128, W], "float32"),
    "in1": ("sbuf", [128, W], "float32"),
}
SEMAPHORES = ["ldd", "lds", "ldm", "y0", "acca", "accb", "gota", "gotb", "sent"]


def rank_program(g, core, T, topo):
    k = core % 8
    r = T.rank_of(core - k)
    if r is None:
        return
    home, mate, peer = T.cores[r], T.cores[r ^ 1], T.cores[r ^ 2]
    S = T.sem

    def tr(dst, srcs, out, mask, rsem):
        rid, pid = topo.addr(dst, core)
        return RemoteDMATransfer(dst_ids=[DstId(rid=rid, pnc=pid)], dma_engine_mask=mask, remote_sem=rsem,
                                 srcs=srcs, dsts=[out], alu_op=1 if len(srcs) > 1 else 0)

    def half(i, base=0):
        return slice(base + i * H, base + (i + 1) * H)

    if k == 0:
        for b, (t, ld) in enumerate(((r ^ 3, S.ldd), (r ^ 2, S.lds), (r ^ 1, S.ldm))):
            g.dma_start(out=T.st[:, b * W:(b + 1) * W], in_=T.x[32 * t:32 * t + 32, :]).then_inc(ld, 16)
        g.wait_ge(S.ldd, 16)
        g.remote_dma_fused([tr(peer + f, [T.st[:, half(i)]], T.in1[:, half(i)], 0xF << (4 * i), S.gotb)
                            for i, f in enumerate(FOLD)], local_sem=S.sent)
        g.wait_ge(S.lds, 16)
        g.remote_dma_fused([tr(home + f, [T.st[:, half(i, W)]], T.in0[:, half(i)], 0xF00 << (4 * i), S.gota)
                            for i, f in enumerate(RELAY)], local_sem=S.sent)
        g.wait_ge(S.ldm, 16)
        g.remote_dma_fused([tr(home + f, [T.st[:, half(i, 2 * W)]], T.in0[:, half(i)], 0xF00 << (4 * i), S.gota)
                            for i, f in enumerate(FOLD)], local_sem=S.sent)
        g.dma_start(out=T.y[:, :], in_=T.x[32 * r:32 * r + 32, :]).then_inc(S.y0, 16)
        g.wait_ge(S.y0, 16)
        g.wait_ge(S.gota, 16)
        g.dma_start(out=T.y[:, :], in_=T.in0[:, :], accum_op=AluOpType.add).then_inc(S.acca, 16)
        g.wait_ge(S.acca, 16)
        g.wait_ge(S.gotb, 16)
        g.dma_start(out=T.y[:, :], in_=T.in1[:, :], accum_op=AluOpType.add).then_inc(S.accb, 16)
        g.wait_ge(S.accb, 16)
        g.wait_ge(S.sent, 24)
    elif k in FOLD:
        c = half(FOLD.index(k))
        g.wait_ge(S.gota, 4)
        g.wait_ge(S.gotb, 4)
        g.remote_dma_fused([tr(mate, [T.in0[:, c], T.in1[:, c]], T.in1[:, c], 0xFF, S.gotb)], local_sem=S.sent)
        g.wait_ge(S.sent, 8)
    elif k in RELAY:
        c = half(RELAY.index(k))
        g.wait_ge(S.gota, 4)
        g.remote_dma_fused([tr(peer, [T.in0[:, c]], T.in0[:, c], 0xFF, S.gota)], local_sem=S.sent)
        g.wait_ge(S.sent, 8)
